import numpy as np
import ml_dtypes


def mxq(x, axis, fmt="e4m3"):
    dtype, down = {"e4m3": (ml_dtypes.float8_e4m3fn, 7), "e5m2": (ml_dtypes.float8_e5m2, 14)}[fmt]
    v = np.moveaxis(np.asarray(x, np.float32).astype(ml_dtypes.bfloat16).astype(np.float64), axis, -1)
    blocks = v.reshape(v.shape[:-1] + (-1, 32))
    amax = np.abs(blocks).max(-1, keepdims=True)
    byte = np.maximum(np.where(amax > 0, np.frexp(amax)[1] - 1 + 127, 0) - down, 1)
    scale = np.exp2(byte - 127.0)
    codes = (blocks / scale).astype(np.float32).astype(dtype).astype(np.float64)
    return np.moveaxis((codes * scale).reshape(v.shape), -1, axis)


WIDE = False


def mx_kscale(k):
    if not WIDE:
        return np.ones(k)
    levels = np.array([10, -10, 5, -5, 0])
    if k % 512:
        return np.exp2(np.random.permutation(np.resize(levels, k // 32))).repeat(32)
    a = np.empty((k // 512, 16))
    for p in range(k // 512):
        a[p, :8] = np.random.permutation(np.resize(levels, 8))
        for g in range(8):
            far = levels[np.abs(levels - a[p, g]) >= 10]
            a[p, g + 8] = far[np.random.randint(len(far))]
    return np.exp2(a.ravel()).repeat(32)


def f64(x):
    return np.asarray(x).astype(np.float64)


def striped(idx):
    return np.tile(np.asarray(idx).reshape(-1, 16).T, (8, 1)).astype(np.uint16)


def unstriped(offs):
    return offs[:16].T.reshape(-1).astype(np.int64)


B, N, T, D, DV, NQ = 4, 512, 4096, 512, 128, 128


def setup_inputs():
    n = np.random.standard_normal
    seg = T // B
    idx = np.concatenate([b * seg + np.random.permutation(seg)[:N] for b in range(B)])
    s = mx_kscale(D)[:, None]
    u = np.ones(T)
    u[idx] = mx_kscale(B * N)
    r = np.random.uniform(0.5, 2.0, T)
    rk = np.random.uniform(0.5, 2.0, T)
    k = n((D, T)) / s / rk
    v = n((DV, T)) / (u * r)
    return {
        "qT": (n((B, D, NQ)) * s * (1.00 / np.sqrt(D))).astype(np.float32),
        "kT": k.astype(np.float32),
        "vT": v.astype(np.float32),
        "ks": np.tile(rk, (128, 1)).astype(np.float32),
        "vs": np.tile(u * r, (128, 1)).astype(np.float32),
        "offs": striped(idx),
    }


def reference(qT, kT, vT, ks, vs, offs):
    idx = unstriped(offs)
    k = f64(kT)
    v = f64(vT)
    pick = lambda x: x[:, idx].reshape(x.shape[0], B, N).transpose(1, 0, 2)
    q = f64(qT)
    score = mxq(q, 1, "e4m3").transpose(0, 2, 1) @ mxq(pick(k), 1, "e4m3")
    score = score * pick(f64(ks))[:, :1, :]
    m = score.max(-1, keepdims=True)
    p = np.exp(score - m)
    total = p.sum(-1, keepdims=True)
    w = p * pick(f64(vs))[:, :1, :]
    y = mxq(w, 2, "e4m3") @ mxq(pick(v).transpose(0, 2, 1), 1, "e4m3")
    y = y / total
    return y

@@ -1,0 +1,267 @@
+from contextlib import ExitStack
+
+import concourse.mybir as mybir
+from concourse.masks import make_identity
+
+F32 = mybir.dt.float32
+BF16 = mybir.dt.bfloat16
+U32 = mybir.dt.uint32
+U16 = mybir.dt.uint16
+U8 = mybir.dt.uint8
+FP8X4 = mybir.dt.float8_e4m3fn_x4
+
+P = 128
+B, N, T, D, DV, NQ = 4, 512, 4096, 512, 128, 128
+SEG = T // B
+COLS = N // 16
+RING = 4
+FLOPS = 2 * B * NQ * N * (D + DV)
+
+COPY = mybir.ActivationFunctionType.Copy
+EXP = mybir.ActivationFunctionType.Exp
+MULT = mybir.AluOpType.mult
+ADD = mybir.AluOpType.add
+MIN = mybir.AluOpType.min
+
+
+def tile_attend_mqa_seg_ks_kernel(tc, qT, kT, vT, ks, vs, offs, out):
+    nc = tc.nc
+    with ExitStack() as ctx:
+        held = ctx.enter_context(tc.tile_pool(name="held", bufs=1))
+        stage = ctx.enter_context(tc.tile_pool(name="stage", bufs=12))
+        ring = ctx.enter_context(tc.tile_pool(name="ring", bufs=RING))
+        work = ctx.enter_context(tc.tile_pool(name="work", bufs=2))
+        deep = ctx.enter_context(tc.tile_pool(name="deep", bufs=4))
+        psum1 = ctx.enter_context(tc.psum_pool(name="psum1", bufs=1))
+        psum2 = ctx.enter_context(tc.psum_pool(name="psum2", bufs=2))
+
+        offsets = held.tile([P, B * COLS], U16, name="offsets")
+        nc.sync.dma_start(offsets[:], offs)
+
+        k_pair = [
+            [held.tile([P, 2 * SEG * (3 + par)], BF16, name=f"k_pair{par}{h}") for h in range(2)] for par in range(2)
+        ]
+        v_raw = [held.tile([P, T // 2], F32, name="v_raw0"), held.tile([P, T], F32, name="v_raw1")]
+        ks_row = [held.tile([P, SEG], F32, name="ks_row0"), held.tile([P, T], F32, name="ks_row1")]
+        vs_row = [held.tile([P, SEG], F32, name="vs_row0"), held.tile([P, T], F32, name="vs_row1")]
+        q_raw = [held.tile([P, 4, NQ], F32, name=f"q_raw{b}") for b in range(B)]
+        ident = held.tile([P, P], F32, name="ident")
+        warm = held.tile([P, 1], F32, name="warm")
+
+        nc.vector.memset(warm[:], 0.0)
+        nc.scalar.activation(warm[:], warm[:], EXP)
+        nc.vector.memset(ks_row[0][64:P, :], 0.0)
+        nc.gpsimd.memset(ks_row[0][32:64, :], 0.0)
+        make_identity(nc, ident[:])
+        nc.vector.memset(vs_row[0][64:P, :], 0.0)
+        nc.gpsimd.memset(vs_row[0][32:64, :], 0.0)
+        for tile, row in ((ks_row[1], ks), (vs_row[1], vs)):
+            nc.gpsimd.memset(tile[:, SEG:T], 0.0)
+            nc.gpsimd.dma_start(tile[0:1, SEG:T], row[0:1, SEG:T])
+
+        k_raw = {}
+
+        def load_q(b):
+            nc.sync.dma_start(q_raw[b][:], qT[b].rearrange("(p j) n -> p j n", j=4))
+
+        def load_k(b, h, i):
+            rows = kT.rearrange("(p j) t -> p j t", j=4)
+            c = b * SEG + i * 512
+            k_raw[b, h, i] = stage.tile([P, 2, 512], F32, name="k_raw")
+            nc.sync.dma_start(k_raw[b, h, i][:], rows[:, 2 * h : 2 * h + 2, c : c + 512])
+
+        load_q(0)
+        nc.sync.dma_start(ks_row[0][0:32, :], ks[0:32, 0:SEG])
+        for i in range(4):
+            load_k(0, i // 2, i % 2)
+        nc.sync.dma_start(vs_row[0][0:32, :], vs[0:32, 0:SEG])
+        load_q(1)
+        for i in range(4):
+            load_k(1, i // 2, i % 2)
+        load_q(2)
+        nc.sync.dma_start(v_raw[0][:], vT[:, 0 : T // 2])
+        for i in range(4):
+            load_k(2, i // 2, i % 2)
+        load_q(3)
+        for i in range(4):
+            load_k(3, i // 2, i % 2)
+        nc.sync.dma_start(v_raw[1][:, T // 2 : T], vT[:, T // 2 : T])
+
+        def slots(b):
+            return offsets[:, b * COLS : (b + 1) * COLS]
+
+        def quantize(x_bf, width, pool, name):
+            codes = pool.tile([P, width], U32, align_bytes=64, name=f"{name}_codes")
+            scales = pool.tile([P, width], U8, align_bytes=64, name=f"{name}_scales")
+            nc.vector.quantize_mx(out=codes[:].bitcast(FP8X4), scales=scales[:], in_=x_bf)
+            return codes, scales
+
+        q, ks_col, vs_col = {}, {}, {}
+        k_mx, scaled, prob, total, v_got, v_bf, v_mx, w_bf, w_mx = {}, {}, {}, {}, {}, {}, {}, {}, {}
+
+        def queries(b):
+            q_bf = deep.tile([P, NQ, 4], BF16, align_bytes=64, name="q_bf")
+            src = q_raw[b][:].rearrange("p j n -> p n j")
+            nc.scalar.activation(q_bf[:], src, COPY)
+            q[b] = quantize(q_bf[:].rearrange("p n j -> p (n j)"), NQ, deep, "q")
+
+        def key_scales(b):
+            got = ring.tile([P, N], F32, align_bytes=64, name="gathered")
+            nc.vector.tensor_copy(got[:], ks_row[min(b, 1)][:].indirect(slots(b)))
+            turned = psum2.tile([P, 4, P], F32, name="scale_turned")
+            for c in range(4):
+                nc.tensor.transpose(turned[:, c, :], got[:, c * P : (c + 1) * P], ident[:])
+            ks_col[b] = deep.tile([P, 4], F32, name="ks_col")
+            nc.scalar.activation(ks_col[b][:], turned[:, :, 0], COPY, scale=-1.0)
+
+        def value_scales(b):
+            got = ring.tile([P, N], F32, align_bytes=64, name="gathered")
+            nc.vector.tensor_copy(got[:], vs_row[min(b, 1)][:].indirect(slots(b)))
+            turned = psum2.tile([P, 4, P], F32, name="scale_turned")
+            for t in range(4):
+                nc.tensor.transpose(turned[:, t, :], got[:, t::4], ident[:])
+            vs_col[b] = deep.tile([P, 1, 4], F32, name="vs_col")
+            nc.scalar.activation(vs_col[b][:, 0, :], turned[:, :, 0], COPY)
+
+        def cast_keys(b, h, halves=(0, 1)):
+            for i in halves:
+                c = i * 512
+                lo = 2 * (b * SEG + c)
+                nc.scalar.activation(
+                    k_pair[b % 2][h][:, lo : lo + 1024].rearrange("p (n e) -> p n e", e=2),
+                    k_raw[b, h, i][:].rearrange("p e n -> p n e"),
+                    COPY,
+                )
+
+        k_bf = {}
+
+        def gather_keys(b, h):
+            if h == 0:
+                k_bf[b] = ring.tile([P, N * 4], BF16, align_bytes=64, name="gathered")
+            words = k_bf[b][:].bitcast(U32).rearrange("p (n h) -> p n h", h=2)
+            table = k_pair[b % 2][h][:, 0 : 2 * (b + 1) * SEG].bitcast(U32)
+            nc.vector.tensor_copy(words[:, :, h], table.indirect(slots(b)))
+
+        def scores(b):
+            k_codes, k_scales = quantize(k_bf[b][:], N, work, "k")
+            q_codes, q_scales = q[b]
+            dots = psum2.tile([P, 4, NQ], F32, name="dots")
+            for c in range(4):
+                cols = slice(c * P, (c + 1) * P)
+                nc.tensor.matmul_mx(
+                    out=dots[:, c, :],
+                    lhsT=k_codes[:, cols].bitcast(FP8X4),
+                    lhsT_scale=k_scales[:, cols],
+                    rhs=q_codes[:].bitcast(FP8X4),
+                    rhs_scale=q_scales[:],
+                    start=True,
+                    stop=True,
+                )
+            scaled[b] = work.tile([P, 4, NQ], F32, name="scaled")
+            for c in range(4):
+                nc.scalar.activation(scaled[b][:, c, :], dots[:, c, :], COPY, scale=ks_col[b][:, c : c + 1])
+
+        score, low = {}, {}
+
+        def turn_scores(b):
+            score[b] = psum1.tile([P, N], F32, name="score")
+            for c in range(4):
+                nc.tensor.transpose(score[b][:, c * P : (c + 1) * P], scaled[b][:, c, :], ident[:])
+
+        def maxima(b):
+            low[b] = deep.tile([P, 1], F32, name="low")
+            nc.vector.tensor_reduce(low[b][:], score[b][:], mybir.AxisListType.X, MIN)
+
+        def exponentials(b):
+            prob[b] = work.tile([P, 4, P], F32, name="prob")
+            total[b] = deep.tile([P, 1], F32, name="total")
+            nc.scalar.activation(
+                prob[b][:],
+                score[b][:].rearrange("p (s t) -> p t s", t=4),
+                EXP,
+                bias=low[b][:],
+                scale=-1.0,
+                accum_out=total[b][:],
+            )
+
+        def gather_values(b):
+            v_got[b] = ring.tile([P, N], F32, align_bytes=64, name="gathered")
+            nc.vector.tensor_copy(v_got[b][:], v_raw[b // 2][:].indirect(slots(b)))
+
+        def turn_values(b):
+            turned = psum1.tile([P, 4, DV], F32, name="v_turned")
+            for t in range(4):
+                nc.tensor.transpose(turned[:, t, :], v_got[b][:, t::4], ident[:])
+            v_bf[b] = work.tile([P, DV, 4], BF16, align_bytes=64, name="v_bf")
+            nc.scalar.activation(v_bf[b][:], turned[:].rearrange("p t e -> p e t"), COPY)
+
+        def quantize_values(b):
+            v_mx[b] = quantize(v_bf[b][:].rearrange("p e t -> p (e t)"), DV, work, "v")
+
+        def weigh(b):
+            turned = psum1.tile([P, 4, NQ], F32, name="w_turned")
+            for t in range(4):
+                nc.tensor.transpose(turned[:, t, :], prob[b][:, t, :], ident[:])
+            w_bf[b] = work.tile([P, NQ, 4], BF16, align_bytes=64, name="w_bf")
+            nc.vector.tensor_tensor(
+                w_bf[b][:], turned[:].rearrange("p t n -> p n t"), vs_col[b][:].to_broadcast([P, NQ, 4]), MULT
+            )
+
+        def quantize_weights(b):
+            w_mx[b] = quantize(w_bf[b][:].rearrange("p n t -> p (n t)"), NQ, work, "w")
+
+        def mix(b):
+            w_codes, w_scales = w_mx[b]
+            v_codes, v_scales = v_mx[b]
+            inverse = deep.tile([P, 1], F32, name="inverse")
+            nc.vector.reciprocal(inverse[:], total[b][:])
+            mixed = psum1.tile([P, DV], F32, name="mixed")
+            nc.tensor.matmul_mx(
+                out=mixed[:],
+                lhsT=w_codes[:].bitcast(FP8X4),
+                lhsT_scale=w_scales[:],
+                rhs=v_codes[:].bitcast(FP8X4),
+                rhs_scale=v_scales[:],
+                start=True,
+                stop=True,
+            )
+            y = work.tile([P, DV], F32, name="y")
+            nc.scalar.activation(y[:], mixed[:], COPY, scale=inverse[:])
+            nc.sync.dma_start(out[b], y[:])
+
+        queries(0)
+        key_scales(0)
+        cast_keys(0, 0)
+        cast_keys(0, 1)
+        gather_keys(0, 0)
+        gather_keys(0, 1)
+        key_scales(1)
+        value_scales(0)
+        for b in range(B):
+            more = b < B - 1
+            if b:
+                gather_keys(b, 0)
+                gather_keys(b, 1)
+            scores(b)
+            turn_scores(b)
+            maxima(b)
+            exponentials(b)
+            if more:
+                queries(b + 1)
+                cast_keys(b + 1, 0)
+                cast_keys(b + 1, 1)
+            if b:
+                weigh(b - 1)
+                quantize_weights(b - 1)
+                quantize_values(b - 1)
+                mix(b - 1)
+            if 0 < b < B - 1:
+                key_scales(b + 1)
+                value_scales(b)
+            gather_values(b)
+            turn_values(b)
+        value_scales(B - 1)
+        weigh(B - 1)
+        quantize_weights(B - 1)
+        quantize_values(B - 1)
+        mix(B - 1)

@@ -14,7 +14,150 @@ P = 128
 B, N, T, D, DV, NQ = 4, 512, 4096, 512, 128, 128
 SEG = T // B
 COLS = N // 16
-RING = 4
+Q_ON_G = (1, 2, 3)
+A_ON_V = ()
+ORDER = (
+    ("L", 0, 0, 0,),
+    ("LV", 0,),
+    ("L", 0, 1, 1,),
+    ("LKS", 2,),
+    ("LVS", 1,),
+    ("L", 0, 1, 0,),
+    ("L", 0, 0, 1,),
+    ("A", 0, 1, 1,),
+    ("LKS", 1,),
+    ("LVS", 0,),
+    ("A", 0, 1, 0,),
+    ("L", 1, 0, 0,),
+    ("L", 3, 0, 1,),
+    ("L", 1, 0, 1,),
+    ("L", 2, 1, 0,),
+    ("L", 1, 1, 1,),
+    ("LKS", 0,),
+    ("LQ", 0,),
+    ("L", 1, 1, 0,),
+    ("A", 0, 0, 1,),
+    ("KSg", 2,),
+    ("A", 0, 0, 0,),
+    ("KG", 0, 0,),
+    ("L", 3, 1, 0,),
+    ("KSt", 2,),
+    ("L", 2, 0, 1,),
+    ("KSg", 0,),
+    ("A", 1, 1, 1,),
+    ("A", 3, 0, 1,),
+    ("LV", 1,),
+    ("A", 1, 0, 1,),
+    ("L", 3, 0, 0,),
+    ("L", 2, 0, 0,),
+    ("A", 1, 0, 0,),
+    ("LQ", 1,),
+    ("LKS", 3,),
+    ("KSg", 3,),
+    ("L", 3, 1, 1,),
+    ("KG", 0, 1,),
+    ("L", 2, 1, 1,),
+    ("A", 3, 1, 0,),
+    ("LQ", 3,),
+    ("KSt", 3,),
+    ("KSt", 0,),
+    ("Qc", 0,),
+    ("KG", 1, 0,),
+    ("LVS", 2,),
+    ("LQ", 2,),
+    ("VSg", 0,),
+    ("A", 2, 0, 0,),
+    ("KQ", 0,),
+    ("LV", 2,),
+    ("VSg", 1,),
+    ("VG", 1,),
+    ("A", 1, 1, 0,),
+    ("A", 3, 0, 0,),
+    ("Qc", 1,),
+    ("Qc", 2,),
+    ("A", 2, 0, 1,),
+    ("Qq", 0,),
+    ("A", 3, 1, 1,),
+    ("KSg", 1,),
+    ("KG", 1, 1,),
+    ("KG", 3, 0,),
+    ("KG", 2, 0,),
+    ("A", 2, 1, 0,),
+    ("MM", 0,),
+    ("A", 2, 1, 1,),
+    ("KQ", 1,),
+    ("KSt", 1,),
+    ("LV", 3,),
+    ("KG", 2, 1,),
+    ("Qc", 3,),
+    ("SC", 0,),
+    ("Qq", 1,),
+    ("MM", 1,),
+    ("Qq", 3,),
+    ("AT", 0,),
+    ("VG", 2,),
+    ("VG", 0,),
+    ("MAX", 0,),
+    ("SC", 1,),
+    ("EX", 0,),
+    ("KG", 3, 1,),
+    ("KQ", 3,),
+    ("Qq", 2,),
+    ("KQ", 2,),
+    ("MM", 2,),
+    ("VSt", 1,),
+    ("REC", 0,),
+    ("VSt", 0,),
+    ("MM", 3,),
+    ("SC", 2,),
+    ("VT", 2,),
+    ("PT", 0,),
+    ("AT", 1,),
+    ("AT", 2,),
+    ("VSg", 2,),
+    ("SC", 3,),
+    ("VG", 3,),
+    ("MAX", 1,),
+    ("EX", 1,),
+    ("VT", 0,),
+    ("WM", 0,),
+    ("VQ", 0,),
+    ("VT", 3,),
+    ("PT", 1,),
+    ("MAX", 2,),
+    ("VT", 1,),
+    ("EX", 2,),
+    ("AT", 3,),
+    ("VSt", 2,),
+    ("REC", 1,),
+    ("WM", 1,),
+    ("MAX", 3,),
+    ("LVS", 3,),
+    ("WQ", 1,),
+    ("WQ", 0,),
+    ("PT", 2,),
+    ("VQ", 3,),
+    ("EX", 3,),
+    ("WM", 2,),
+    ("VSg", 3,),
+    ("M2", 0,),
+    ("VQ", 1,),
+    ("Y", 0,),
+    ("VQ", 2,),
+    ("WQ", 2,),
+    ("VSt", 3,),
+    ("REC", 3,),
+    ("M2", 2,),
+    ("PT", 3,),
+    ("WM", 3,),
+    ("REC", 2,),
+    ("Y", 2,),
+    ("WQ", 3,),
+    ("M2", 1,),
+    ("Y", 1,),
+    ("M2", 3,),
+    ("Y", 3,),
+)
 FLOPS = 2 * B * NQ * N * (D + DV)
 
 COPY = mybir.ActivationFunctionType.Copy
@@ -28,9 +171,10 @@ def tile_attend_mqa_seg_ks_kernel(tc, qT, kT, vT, ks, vs, offs, out):
     nc = tc.nc
     with ExitStack() as ctx:
         held = ctx.enter_context(tc.tile_pool(name="held", bufs=1))
-        stage = ctx.enter_context(tc.tile_pool(name="stage", bufs=12))
-        ring = ctx.enter_context(tc.tile_pool(name="ring", bufs=RING))
-        work = ctx.enter_context(tc.tile_pool(name="work", bufs=2))
+        stage = ctx.enter_context(tc.tile_pool(name="stage", bufs=14))
+        pair = ctx.enter_context(tc.tile_pool(name="pair", bufs=4))
+        ring = ctx.enter_context(tc.tile_pool(name="ring", bufs=4))
+        work = ctx.enter_context(tc.tile_pool(name="work", bufs=4))
         deep = ctx.enter_context(tc.tile_pool(name="deep", bufs=4))
         psum1 = ctx.enter_context(tc.psum_pool(name="psum1", bufs=1))
         psum2 = ctx.enter_context(tc.psum_pool(name="psum2", bufs=2))
@@ -38,26 +182,23 @@ def tile_attend_mqa_seg_ks_kernel(tc, qT, kT, vT, ks, vs, offs, out):
         offsets = held.tile([P, B * COLS], U16, name="offsets")
         nc.sync.dma_start(offsets[:], offs)
 
-        k_pair = [
-            [held.tile([P, 2 * SEG * (3 + par)], BF16, name=f"k_pair{par}{h}") for h in range(2)] for par in range(2)
-        ]
-        v_raw = [held.tile([P, T // 2], F32, name="v_raw0"), held.tile([P, T], F32, name="v_raw1")]
-        ks_row = [held.tile([P, SEG], F32, name="ks_row0"), held.tile([P, T], F32, name="ks_row1")]
-        vs_row = [held.tile([P, SEG], F32, name="vs_row0"), held.tile([P, T], F32, name="vs_row1")]
+        k_pair = [held.tile([P, 2 * T], BF16, name=f"k_pair{h}") for h in range(2)]
+        v_raw = held.tile([P, T], F32, name="v_raw")
+        ks_row = held.tile([P, T], F32, name="ks_row")
+        vs_row = held.tile([P, T], F32, name="vs_row")
         q_raw = [held.tile([P, 4, NQ], F32, name=f"q_raw{b}") for b in range(B)]
         ident = held.tile([P, P], F32, name="ident")
         warm = held.tile([P, 1], F32, name="warm")
 
         nc.vector.memset(warm[:], 0.0)
         nc.scalar.activation(warm[:], warm[:], EXP)
-        nc.vector.memset(ks_row[0][64:P, :], 0.0)
-        nc.gpsimd.memset(ks_row[0][32:64, :], 0.0)
+        nc.vector.memset(ks_row[:, 0:SEG], 0.0)
+        nc.vector.memset(vs_row[:, 0:SEG], 0.0)
+        nc.gpsimd.memset(ks_row[:, SEG : 2 * SEG], 0.0)
         make_identity(nc, ident[:])
-        nc.vector.memset(vs_row[0][64:P, :], 0.0)
-        nc.gpsimd.memset(vs_row[0][32:64, :], 0.0)
-        for tile, row in ((ks_row[1], ks), (vs_row[1], vs)):
-            nc.gpsimd.memset(tile[:, SEG:T], 0.0)
-            nc.gpsimd.dma_start(tile[0:1, SEG:T], row[0:1, SEG:T])
+        nc.gpsimd.memset(vs_row[:, SEG : 2 * SEG], 0.0)
+        nc.gpsimd.memset(ks_row[:, 2 * SEG : T], 0.0)
+        nc.gpsimd.memset(vs_row[:, 2 * SEG : T], 0.0)
 
         k_raw = {}
 
@@ -70,22 +211,14 @@ def tile_attend_mqa_seg_ks_kernel(tc, qT, kT, vT, ks, vs, offs, out):
             k_raw[b, h, i] = stage.tile([P, 2, 512], F32, name="k_raw")
             nc.sync.dma_start(k_raw[b, h, i][:], rows[:, 2 * h : 2 * h + 2, c : c + 512])
 
-        load_q(0)
-        nc.sync.dma_start(ks_row[0][0:32, :], ks[0:32, 0:SEG])
-        for i in range(4):
-            load_k(0, i // 2, i % 2)
-        nc.sync.dma_start(vs_row[0][0:32, :], vs[0:32, 0:SEG])
-        load_q(1)
-        for i in range(4):
-            load_k(1, i // 2, i % 2)
-        load_q(2)
-        nc.sync.dma_start(v_raw[0][:], vT[:, 0 : T // 2])
-        for i in range(4):
-            load_k(2, i // 2, i % 2)
-        load_q(3)
-        for i in range(4):
-            load_k(3, i // 2, i % 2)
-        nc.sync.dma_start(v_raw[1][:, T // 2 : T], vT[:, T // 2 : T])
+        def load_key_scales(b):
+            nc.sync.dma_start(ks_row[0:1, b * SEG : (b + 1) * SEG], ks[0:1, b * SEG : (b + 1) * SEG])
+
+        def load_value_scales(b):
+            nc.sync.dma_start(vs_row[0:1, b * SEG : (b + 1) * SEG], vs[0:1, b * SEG : (b + 1) * SEG])
+
+        def load_v(b):
+            nc.sync.dma_start(v_raw[:, b * SEG : (b + 1) * SEG], vT[:, b * SEG : (b + 1) * SEG])
 
         def slots(b):
             return offsets[:, b * COLS : (b + 1) * COLS]
@@ -99,25 +232,41 @@ def tile_attend_mqa_seg_ks_kernel(tc, qT, kT, vT, ks, vs, offs, out):
         q, ks_col, vs_col = {}, {}, {}
         k_mx, scaled, prob, total, v_got, v_bf, v_mx, w_bf, w_mx = {}, {}, {}, {}, {}, {}, {}, {}, {}
 
-        def queries(b):
-            q_bf = deep.tile([P, NQ, 4], BF16, align_bytes=64, name="q_bf")
+        q_bfs = {}
+
+        def cast_queries(b):
+            q_bf = q_bfs[b] = deep.tile([P, NQ, 4], BF16, align_bytes=64, name="q_bf")
             src = q_raw[b][:].rearrange("p j n -> p n j")
-            nc.scalar.activation(q_bf[:], src, COPY)
+            if b in Q_ON_G:
+                nc.gpsimd.tensor_scalar(q_bf[:], src, 1.0, 0.0, MULT, ADD)
+            else:
+                nc.scalar.activation(q_bf[:], src, COPY)
+
+        def quantize_queries(b):
+            q_bf = q_bfs[b]
             q[b] = quantize(q_bf[:].rearrange("p n j -> p (n j)"), NQ, deep, "q")
 
+        row_got = {}
+
         def key_scales(b):
-            got = ring.tile([P, N], F32, align_bytes=64, name="gathered")
-            nc.vector.tensor_copy(got[:], ks_row[min(b, 1)][:].indirect(slots(b)))
-            turned = psum2.tile([P, 4, P], F32, name="scale_turned")
+            got = row_got["k", b] = pair.tile([P, N], F32, name="row_got")
+            nc.vector.tensor_copy(got[:], ks_row[:, 0 : (b + 1) * SEG].indirect(slots(b)))
+
+        def key_column(b):
+            got = row_got["k", b]
+            turned = psum1.tile([P, 4, P], F32, name="scale_turned")
             for c in range(4):
                 nc.tensor.transpose(turned[:, c, :], got[:, c * P : (c + 1) * P], ident[:])
             ks_col[b] = deep.tile([P, 4], F32, name="ks_col")
             nc.scalar.activation(ks_col[b][:], turned[:, :, 0], COPY, scale=-1.0)
 
         def value_scales(b):
-            got = ring.tile([P, N], F32, align_bytes=64, name="gathered")
-            nc.vector.tensor_copy(got[:], vs_row[min(b, 1)][:].indirect(slots(b)))
-            turned = psum2.tile([P, 4, P], F32, name="scale_turned")
+            got = row_got["v", b] = pair.tile([P, N], F32, name="row_got")
+            nc.vector.tensor_copy(got[:], vs_row[:, 0 : (b + 1) * SEG].indirect(slots(b)))
+
+        def value_column(b):
+            got = row_got["v", b]
+            turned = psum1.tile([P, 4, P], F32, name="scale_turned")
             for t in range(4):
                 nc.tensor.transpose(turned[:, t, :], got[:, t::4], ident[:])
             vs_col[b] = deep.tile([P, 1, 4], F32, name="vs_col")
@@ -127,23 +276,27 @@ def tile_attend_mqa_seg_ks_kernel(tc, qT, kT, vT, ks, vs, offs, out):
             for i in halves:
                 c = i * 512
                 lo = 2 * (b * SEG + c)
-                nc.scalar.activation(
-                    k_pair[b % 2][h][:, lo : lo + 1024].rearrange("p (n e) -> p n e", e=2),
+                copy = nc.scalar.activation if (b, h, i) not in A_ON_V else lambda o, s, f: nc.vector.tensor_copy(o, s)
+                copy(
+                    k_pair[h][:, lo : lo + 1024].rearrange("p (n e) -> p n e", e=2),
                     k_raw[b, h, i][:].rearrange("p e n -> p n e"),
                     COPY,
                 )
 
-        k_bf = {}
+        k_bf, all_dots, w_turned, mixes = {}, {}, {}, {}
 
         def gather_keys(b, h):
             if h == 0:
                 k_bf[b] = ring.tile([P, N * 4], BF16, align_bytes=64, name="gathered")
             words = k_bf[b][:].bitcast(U32).rearrange("p (n h) -> p n h", h=2)
-            table = k_pair[b % 2][h][:, 0 : 2 * (b + 1) * SEG].bitcast(U32)
+            table = k_pair[h][:, 0 : 2 * (b + 1) * SEG].bitcast(U32)
             nc.vector.tensor_copy(words[:, :, h], table.indirect(slots(b)))
 
+        def quantize_keys(b):
+            k_mx[b] = quantize(k_bf[b][:], N, work, "k")
+
         def scores(b):
-            k_codes, k_scales = quantize(k_bf[b][:], N, work, "k")
+            k_codes, k_scales = k_mx[b]
             q_codes, q_scales = q[b]
             dots = psum2.tile([P, 4, NQ], F32, name="dots")
             for c in range(4):
@@ -157,6 +310,10 @@ def tile_attend_mqa_seg_ks_kernel(tc, qT, kT, vT, ks, vs, offs, out):
                     start=True,
                     stop=True,
                 )
+            all_dots[b] = dots
+
+        def scale_scores(b):
+            dots = all_dots[b]
             scaled[b] = work.tile([P, 4, NQ], F32, name="scaled")
             for c in range(4):
                 nc.scalar.activation(scaled[b][:, c, :], dots[:, c, :], COPY, scale=ks_col[b][:, c : c + 1])
@@ -164,7 +321,7 @@ def tile_attend_mqa_seg_ks_kernel(tc, qT, kT, vT, ks, vs, offs, out):
         score, low = {}, {}
 
         def turn_scores(b):
-            score[b] = psum1.tile([P, N], F32, name="score")
+            score[b] = psum2.tile([P, N], F32, name="score")
             for c in range(4):
                 nc.tensor.transpose(score[b][:, c * P : (c + 1) * P], scaled[b][:, c, :], ident[:])
 
@@ -185,8 +342,8 @@ def tile_attend_mqa_seg_ks_kernel(tc, qT, kT, vT, ks, vs, offs, out):
             )
 
         def gather_values(b):
-            v_got[b] = ring.tile([P, N], F32, align_bytes=64, name="gathered")
-            nc.vector.tensor_copy(v_got[b][:], v_raw[b // 2][:].indirect(slots(b)))
+            v_got[b] = pair.tile([P, N], F32, name="v_got")
+            nc.vector.tensor_copy(v_got[b][:], v_raw[:, 0 : (b + 1) * SEG].indirect(slots(b)))
 
         def turn_values(b):
             turned = psum1.tile([P, 4, DV], F32, name="v_turned")
@@ -198,10 +355,13 @@ def tile_attend_mqa_seg_ks_kernel(tc, qT, kT, vT, ks, vs, offs, out):
         def quantize_values(b):
             v_mx[b] = quantize(v_bf[b][:].rearrange("p e t -> p (e t)"), DV, work, "v")
 
-        def weigh(b):
-            turned = psum1.tile([P, 4, NQ], F32, name="w_turned")
+        def turn_weights(b):
+            turned = w_turned[b] = psum1.tile([P, 4, NQ], F32, name="w_turned")
             for t in range(4):
                 nc.tensor.transpose(turned[:, t, :], prob[b][:, t, :], ident[:])
+
+        def weigh(b):
+            turned = w_turned[b]
             w_bf[b] = work.tile([P, NQ, 4], BF16, align_bytes=64, name="w_bf")
             nc.vector.tensor_tensor(
                 w_bf[b][:], turned[:].rearrange("p t n -> p n t"), vs_col[b][:].to_broadcast([P, NQ, 4]), MULT
@@ -213,8 +373,6 @@ def tile_attend_mqa_seg_ks_kernel(tc, qT, kT, vT, ks, vs, offs, out):
         def mix(b):
             w_codes, w_scales = w_mx[b]
             v_codes, v_scales = v_mx[b]
-            inverse = deep.tile([P, 1], F32, name="inverse")
-            nc.vector.reciprocal(inverse[:], total[b][:])
             mixed = psum1.tile([P, DV], F32, name="mixed")
             nc.tensor.matmul_mx(
                 out=mixed[:],
@@ -225,43 +383,26 @@ def tile_attend_mqa_seg_ks_kernel(tc, qT, kT, vT, ks, vs, offs, out):
                 start=True,
                 stop=True,
             )
+            mixes[b] = mixed
+
+        inverses = {}
+
+        def invert(b):
+            inverse = inverses[b] = deep.tile([P, 1], F32, name="inverse")
+            nc.vector.reciprocal(inverse[:], total[b][:])
+
+        def finish(b):
+            inverse, mixed = inverses[b], mixes[b]
             y = work.tile([P, DV], F32, name="y")
             nc.scalar.activation(y[:], mixed[:], COPY, scale=inverse[:])
             nc.sync.dma_start(out[b], y[:])
 
-        queries(0)
-        key_scales(0)
-        cast_keys(0, 0)
-        cast_keys(0, 1)
-        gather_keys(0, 0)
-        gather_keys(0, 1)
-        key_scales(1)
-        value_scales(0)
-        for b in range(B):
-            more = b < B - 1
-            if b:
-                gather_keys(b, 0)
-                gather_keys(b, 1)
-            scores(b)
-            turn_scores(b)
-            maxima(b)
-            exponentials(b)
-            if more:
-                queries(b + 1)
-                cast_keys(b + 1, 0)
-                cast_keys(b + 1, 1)
-            if b:
-                weigh(b - 1)
-                quantize_weights(b - 1)
-                quantize_values(b - 1)
-                mix(b - 1)
-            if 0 < b < B - 1:
-                key_scales(b + 1)
-                value_scales(b)
-            gather_values(b)
-            turn_values(b)
-        value_scales(B - 1)
-        weigh(B - 1)
-        quantize_weights(B - 1)
-        quantize_values(B - 1)
-        mix(B - 1)
+        units = {
+            "L": load_k, "LQ": load_q, "LKS": load_key_scales, "LVS": load_value_scales, "LV": load_v,
+            "Qc": cast_queries, "Qq": quantize_queries, "KSg": key_scales, "KSt": key_column, "VSg": value_scales,
+            "VSt": value_column, "A": lambda b, h, i: cast_keys(b, h, (i,)), "KG": gather_keys, "KQ": quantize_keys, "MM": scores,
+            "SC": scale_scores, "AT": turn_scores, "MAX": maxima, "EX": exponentials, "VG": gather_values, "VT": turn_values, "VQ": quantize_values, "PT": turn_weights, "WM": weigh,
+            "WQ": quantize_weights, "REC": invert, "M2": mix, "Y": finish,
+        }
+        for u in ORDER:
+            units[u[0]](*u[1:])

@@ -16,145 +16,144 @@ SEG = T // B
 COLS = N // 16
 Q_ON_G = (1, 2, 3)
 A_ON_V = ()
+IL_ON_S = ()
 ORDER = (
-    ("L", 0, 0, 0,),
-    ("LV", 0,),
-    ("L", 0, 1, 1,),
-    ("LKS", 2,),
-    ("LVS", 1,),
-    ("L", 0, 1, 0,),
-    ("L", 0, 0, 1,),
-    ("A", 0, 1, 1,),
-    ("LKS", 1,),
-    ("LVS", 0,),
-    ("A", 0, 1, 0,),
-    ("L", 1, 0, 0,),
-    ("L", 3, 0, 1,),
-    ("L", 1, 0, 1,),
-    ("L", 2, 1, 0,),
-    ("L", 1, 1, 1,),
-    ("LKS", 0,),
-    ("LQ", 0,),
-    ("L", 1, 1, 0,),
-    ("A", 0, 0, 1,),
-    ("KSg", 2,),
-    ("A", 0, 0, 0,),
-    ("KG", 0, 0,),
-    ("L", 3, 1, 0,),
-    ("KSt", 2,),
-    ("L", 2, 0, 1,),
-    ("KSg", 0,),
-    ("A", 1, 1, 1,),
-    ("A", 3, 0, 1,),
-    ("LV", 1,),
-    ("A", 1, 0, 1,),
-    ("L", 3, 0, 0,),
-    ("L", 2, 0, 0,),
-    ("A", 1, 0, 0,),
     ("LQ", 1,),
     ("LKS", 3,),
-    ("KSg", 3,),
-    ("L", 3, 1, 1,),
-    ("KG", 0, 1,),
-    ("L", 2, 1, 1,),
-    ("A", 3, 1, 0,),
     ("LQ", 3,),
-    ("KSt", 3,),
-    ("KSt", 0,),
-    ("Qc", 0,),
-    ("KG", 1, 0,),
-    ("LVS", 2,),
+    ("LKS", 0,),
+    ("LV", 0,),
+    ("LKS", 2,),
+    ("LQ", 0,),
+    ("LV", 1,),
     ("LQ", 2,),
-    ("VSg", 0,),
-    ("A", 2, 0, 0,),
-    ("KQ", 0,),
-    ("LV", 2,),
-    ("VSg", 1,),
-    ("VG", 1,),
-    ("A", 1, 1, 0,),
-    ("A", 3, 0, 0,),
-    ("Qc", 1,),
+    ("L", 0, 1, 1,),
+    ("Qc", 0,),
+    ("LVS", 1,),
     ("Qc", 2,),
-    ("A", 2, 0, 1,),
+    ("LKS", 1,),
+    ("L", 1, 1,),
+    ("LV", 2,),
+    ("LVS", 0,),
+    ("L", 0, 1, 0,),
     ("Qq", 0,),
-    ("A", 3, 1, 1,),
+    ("L", 3, 0,),
+    ("KSg", 0,),
+    ("KSg", 2,),
+    ("A", 3, 0, 0,),
+    ("L", 1, 0,),
+    ("KSt", 0,),
+    ("L", 0, 0, 0,),
+    ("A", 1, 0, 0,),
     ("KSg", 1,),
+    ("A", 0, 1, 1,),
+    ("LV", 3,),
+    ("L", 0, 0, 1,),
+    ("A", 0, 1, 0,),
+    ("KSt", 1,),
+    ("A", 1, 0, 1,),
+    ("A", 3, 0, 1,),
+    ("LVS", 2,),
+    ("A", 0, 0, 0,),
+    ("L", 2, 0,),
+    ("A", 0, 0, 1,),
+    ("Qq", 2,),
+    ("A", 1, 1, 0,),
+    ("Qc", 3,),
+    ("A", 2, 0, 0,),
+    ("VG", 2,),
+    ("VSg", 2,),
+    ("KG", 0, 0,),
+    ("KSt", 2,),
+    ("A", 1, 1, 1,),
+    ("KG", 1, 0,),
     ("KG", 1, 1,),
-    ("KG", 3, 0,),
+    ("Qq", 3,),
+    ("LVS", 3,),
+    ("VSg", 0,),
+    ("VSg", 1,),
+    ("A", 2, 0, 1,),
+    ("KG", 0, 1,),
+    ("L", 2, 1,),
+    ("A", 2, 1, 1,),
     ("KG", 2, 0,),
     ("A", 2, 1, 0,),
-    ("MM", 0,),
-    ("A", 2, 1, 1,),
-    ("KQ", 1,),
-    ("KSt", 1,),
-    ("LV", 3,),
+    ("L", 3, 1,),
     ("KG", 2, 1,),
-    ("Qc", 3,),
-    ("SC", 0,),
+    ("IL", 0,),
+    ("Qc", 1,),
+    ("IL", 1,),
+    ("IL", 2,),
+    ("KQ", 0,),
+    ("VG", 1,),
+    ("KQ", 1,),
+    ("KG", 3, 0,),
     ("Qq", 1,),
-    ("MM", 1,),
-    ("Qq", 3,),
-    ("AT", 0,),
-    ("VG", 2,),
-    ("VG", 0,),
-    ("MAX", 0,),
-    ("SC", 1,),
-    ("EX", 0,),
-    ("KG", 3, 1,),
-    ("KQ", 3,),
-    ("Qq", 2,),
     ("KQ", 2,),
-    ("MM", 2,),
-    ("VSt", 1,),
-    ("REC", 0,),
-    ("VSt", 0,),
-    ("MM", 3,),
-    ("SC", 2,),
-    ("VT", 2,),
-    ("PT", 0,),
-    ("AT", 1,),
-    ("AT", 2,),
-    ("VSg", 2,),
-    ("SC", 3,),
-    ("VG", 3,),
-    ("MAX", 1,),
-    ("EX", 1,),
-    ("VT", 0,),
-    ("WM", 0,),
-    ("VQ", 0,),
-    ("VT", 3,),
-    ("PT", 1,),
-    ("MAX", 2,),
-    ("VT", 1,),
-    ("EX", 2,),
-    ("AT", 3,),
     ("VSt", 2,),
-    ("REC", 1,),
-    ("WM", 1,),
-    ("MAX", 3,),
-    ("LVS", 3,),
-    ("WQ", 1,),
-    ("WQ", 0,),
-    ("PT", 2,),
-    ("VQ", 3,),
-    ("EX", 3,),
-    ("WM", 2,),
+    ("A", 3, 1, 1,),
+    ("A", 3, 1, 0,),
+    ("VT", 1,),
+    ("VSt", 1,),
+    ("KSg", 3,),
+    ("MM", 0,),
+    ("KG", 3, 1,),
+    ("MM", 1,),
+    ("VG", 3,),
+    ("VT", 3,),
     ("VSg", 3,),
-    ("M2", 0,),
-    ("VQ", 1,),
-    ("Y", 0,),
-    ("VQ", 2,),
-    ("WQ", 2,),
+    ("VG", 0,),
+    ("SC", 0,),
+    ("MM", 2,),
+    ("AT", 0,),
+    ("VSt", 0,),
+    ("IL", 3,),
+    ("SC", 1,),
     ("VSt", 3,),
-    ("REC", 3,),
-    ("M2", 2,),
+    ("MAX", 0,),
+    ("VT", 2,),
+    ("AT", 1,),
+    ("VQ", 2,),
+    ("VT", 0,),
+    ("SC", 2,),
+    ("VQ", 3,),
+    ("EX", 0,),
+    ("MAX", 1,),
+    ("PT", 0,),
+    ("KSt", 3,),
+    ("EX", 1,),
+    ("WM", 0,),
+    ("PT", 1,),
+    ("KQ", 3,),
+    ("AT", 2,),
+    ("WM", 1,),
+    ("WQ", 0,),
+    ("REC", 1,),
+    ("VQ", 0,),
+    ("WQ", 1,),
+    ("MAX", 2,),
+    ("MM", 3,),
+    ("SC", 3,),
+    ("AT", 3,),
+    ("EX", 2,),
+    ("PT", 2,),
+    ("M2", 0,),
+    ("REC", 0,),
+    ("MAX", 3,),
+    ("WM", 2,),
+    ("EX", 3,),
+    ("WQ", 2,),
+    ("VQ", 1,),
     ("PT", 3,),
-    ("WM", 3,),
+    ("Y", 0,),
     ("REC", 2,),
+    ("M2", 2,),
+    ("WM", 3,),
     ("Y", 2,),
-    ("WQ", 3,),
     ("M2", 1,),
     ("Y", 1,),
+    ("WQ", 3,),
+    ("REC", 3,),
     ("M2", 3,),
     ("Y", 3,),
 )
@@ -171,9 +170,10 @@ def tile_attend_mqa_seg_ks_kernel(tc, qT, kT, vT, ks, vs, offs, out):
     nc = tc.nc
     with ExitStack() as ctx:
         held = ctx.enter_context(tc.tile_pool(name="held", bufs=1))
-        stage = ctx.enter_context(tc.tile_pool(name="stage", bufs=14))
+        first = ctx.enter_context(tc.tile_pool(name="first", bufs=4))
+        stage = ctx.enter_context(tc.tile_pool(name="stage", bufs=6))
         pair = ctx.enter_context(tc.tile_pool(name="pair", bufs=4))
-        ring = ctx.enter_context(tc.tile_pool(name="ring", bufs=4))
+        ring = ctx.enter_context(tc.tile_pool(name="ring", bufs=3))
         work = ctx.enter_context(tc.tile_pool(name="work", bufs=4))
         deep = ctx.enter_context(tc.tile_pool(name="deep", bufs=4))
         psum1 = ctx.enter_context(tc.psum_pool(name="psum1", bufs=1))
@@ -188,6 +188,7 @@ def tile_attend_mqa_seg_ks_kernel(tc, qT, kT, vT, ks, vs, offs, out):
         vs_row = held.tile([P, T], F32, name="vs_row")
         q_raw = [held.tile([P, 4, NQ], F32, name=f"q_raw{b}") for b in range(B)]
         ident = held.tile([P, P], F32, name="ident")
+        ident_bf = held.tile([P, P], BF16, name="ident_bf")
         warm = held.tile([P, 1], F32, name="warm")
 
         nc.vector.memset(warm[:], 0.0)
@@ -196,6 +197,7 @@ def tile_attend_mqa_seg_ks_kernel(tc, qT, kT, vT, ks, vs, offs, out):
         nc.vector.memset(vs_row[:, 0:SEG], 0.0)
         nc.gpsimd.memset(ks_row[:, SEG : 2 * SEG], 0.0)
         make_identity(nc, ident[:])
+        nc.gpsimd.tensor_copy(ident_bf[:], ident[:])
         nc.gpsimd.memset(vs_row[:, SEG : 2 * SEG], 0.0)
         nc.gpsimd.memset(ks_row[:, 2 * SEG : T], 0.0)
         nc.gpsimd.memset(vs_row[:, 2 * SEG : T], 0.0)
@@ -205,11 +207,13 @@ def tile_attend_mqa_seg_ks_kernel(tc, qT, kT, vT, ks, vs, offs, out):
         def load_q(b):
             nc.sync.dma_start(q_raw[b][:], qT[b].rearrange("(p j) n -> p j n", j=4))
 
-        def load_k(b, h, i):
+        def load_k(b, h, i=None):
             rows = kT.rearrange("(p j) t -> p j t", j=4)
-            c = b * SEG + i * 512
-            k_raw[b, h, i] = stage.tile([P, 2, 512], F32, name="k_raw")
-            nc.sync.dma_start(k_raw[b, h, i][:], rows[:, 2 * h : 2 * h + 2, c : c + 512])
+            lo, width = (b * SEG, SEG) if i is None else (b * SEG + i * 512, 512)
+            tile = (stage if i is None else first).tile([P, 2, width], F32, name="k_raw" if i is None else "k_first")
+            nc.sync.dma_start(tile[:], rows[:, 2 * h : 2 * h + 2, lo : lo + width])
+            for j in range(lo, lo + width, 512):
+                k_raw[b, h, j // 512 % 2] = tile[:, :, j - lo : j - lo + 512]
 
         def load_key_scales(b):
             nc.sync.dma_start(ks_row[0:1, b * SEG : (b + 1) * SEG], ks[0:1, b * SEG : (b + 1) * SEG])
@@ -279,18 +283,32 @@ def tile_attend_mqa_seg_ks_kernel(tc, qT, kT, vT, ks, vs, offs, out):
                 copy = nc.scalar.activation if (b, h, i) not in A_ON_V else lambda o, s, f: nc.vector.tensor_copy(o, s)
                 copy(
                     k_pair[h][:, lo : lo + 1024].rearrange("p (n e) -> p n e", e=2),
-                    k_raw[b, h, i][:].rearrange("p e n -> p n e"),
+                    k_raw[b, h, i].rearrange("p e n -> p n e"),
                     COPY,
                 )
 
         k_bf, all_dots, w_turned, mixes = {}, {}, {}, {}
 
+        k_got = {}
+
         def gather_keys(b, h):
             if h == 0:
-                k_bf[b] = ring.tile([P, N * 4], BF16, align_bytes=64, name="gathered")
-            words = k_bf[b][:].bitcast(U32).rearrange("p (n h) -> p n h", h=2)
+                k_got[b] = ring.tile([P, 2, 2 * N], BF16, align_bytes=64, name="k_got")
             table = k_pair[h][:, 0 : 2 * (b + 1) * SEG].bitcast(U32)
-            nc.vector.tensor_copy(words[:, :, h], table.indirect(slots(b)))
+            nc.vector.tensor_copy(k_got[b][:, h, :].bitcast(U32), table.indirect(slots(b)))
+
+        def interleave(b):
+            k_bf[b] = ring.tile([P, N * 4], BF16, align_bytes=64, name="gathered")
+            if b in IL_ON_S:
+                nc.scalar.copy(
+                    k_bf[b][:].rearrange("p (n h e) -> p n h e", h=2, e=2),
+                    k_got[b][:].rearrange("p h (n e) -> p n h e", e=2),
+                )
+            else:
+                nc.vector.tensor_copy(
+                    k_bf[b][:].bitcast(U32).rearrange("p (n h) -> p n h", h=2),
+                    k_got[b][:].rearrange("p h x -> p (h x)").bitcast(U32).rearrange("p (h n) -> p n h", h=2),
+                )
 
         def quantize_keys(b):
             k_mx[b] = quantize(k_bf[b][:], N, work, "k")
@@ -342,15 +360,17 @@ def tile_attend_mqa_seg_ks_kernel(tc, qT, kT, vT, ks, vs, offs, out):
             )
 
         def gather_values(b):
-            v_got[b] = pair.tile([P, N], F32, name="v_got")
-            nc.vector.tensor_copy(v_got[b][:], v_raw[:, 0 : (b + 1) * SEG].indirect(slots(b)))
+            v_got[b] = pair.tile([P, 4, P], BF16, name="v_got")
+            nc.vector.tensor_copy(
+                v_got[b][:].rearrange("p t s -> p s t"), v_raw[:, 0 : (b + 1) * SEG].indirect(slots(b))
+            )
 
         def turn_values(b):
-            turned = psum1.tile([P, 4, DV], F32, name="v_turned")
+            turned = psum1.tile([P, 4, DV], BF16, name="v_turned")
             for t in range(4):
-                nc.tensor.transpose(turned[:, t, :], v_got[b][:, t::4], ident[:])
+                nc.tensor.transpose(turned[:, t, :], v_got[b][:, t, :], ident_bf[:])
             v_bf[b] = work.tile([P, DV, 4], BF16, align_bytes=64, name="v_bf")
-            nc.scalar.activation(v_bf[b][:], turned[:].rearrange("p t e -> p e t"), COPY)
+            nc.scalar.copy(v_bf[b][:], turned[:].rearrange("p t e -> p e t"))
 
         def quantize_values(b):
             v_mx[b] = quantize(v_bf[b][:].rearrange("p e t -> p (e t)"), DV, work, "v")
@@ -400,7 +420,7 @@ def tile_attend_mqa_seg_ks_kernel(tc, qT, kT, vT, ks, vs, offs, out):
         units = {
             "L": load_k, "LQ": load_q, "LKS": load_key_scales, "LVS": load_value_scales, "LV": load_v,
             "Qc": cast_queries, "Qq": quantize_queries, "KSg": key_scales, "KSt": key_column, "VSg": value_scales,
-            "VSt": value_column, "A": lambda b, h, i: cast_keys(b, h, (i,)), "KG": gather_keys, "KQ": quantize_keys, "MM": scores,
+            "VSt": value_column, "A": lambda b, h, i: cast_keys(b, h, (i,)), "KG": gather_keys, "IL": interleave, "KQ": quantize_keys, "MM": scores,
             "SC": scale_scores, "AT": turn_scores, "MAX": maxima, "EX": exponentials, "VG": gather_values, "VT": turn_values, "VQ": quantize_values, "PT": turn_weights, "WM": weigh,
             "WQ": quantize_weights, "REC": invert, "M2": mix, "Y": finish,
         }

@@ -13,150 +13,8 @@ FP8X4 = mybir.dt.float8_e4m3fn_x4
 P = 128
 B, N, T, D, DV, NQ = 4, 512, 4096, 512, 128, 128
 SEG = T // B
+HALF = SEG // 2
 COLS = N // 16
-Q_ON_G = (1, 2, 3)
-A_ON_V = ()
-IL_ON_S = ()
-ORDER = (
-    ("LQ", 1,),
-    ("LKS", 3,),
-    ("LQ", 3,),
-    ("LKS", 0,),
-    ("LV", 0,),
-    ("LKS", 2,),
-    ("LQ", 0,),
-    ("LV", 1,),
-    ("LQ", 2,),
-    ("L", 0, 1, 1,),
-    ("Qc", 0,),
-    ("LVS", 1,),
-    ("Qc", 2,),
-    ("LKS", 1,),
-    ("L", 1, 1,),
-    ("LV", 2,),
-    ("LVS", 0,),
-    ("L", 0, 1, 0,),
-    ("Qq", 0,),
-    ("L", 3, 0,),
-    ("KSg", 0,),
-    ("KSg", 2,),
-    ("A", 3, 0, 0,),
-    ("L", 1, 0,),
-    ("KSt", 0,),
-    ("L", 0, 0, 0,),
-    ("A", 1, 0, 0,),
-    ("KSg", 1,),
-    ("A", 0, 1, 1,),
-    ("LV", 3,),
-    ("L", 0, 0, 1,),
-    ("A", 0, 1, 0,),
-    ("KSt", 1,),
-    ("A", 1, 0, 1,),
-    ("A", 3, 0, 1,),
-    ("LVS", 2,),
-    ("A", 0, 0, 0,),
-    ("L", 2, 0,),
-    ("A", 0, 0, 1,),
-    ("Qq", 2,),
-    ("A", 1, 1, 0,),
-    ("Qc", 3,),
-    ("A", 2, 0, 0,),
-    ("VG", 2,),
-    ("VSg", 2,),
-    ("KG", 0, 0,),
-    ("KSt", 2,),
-    ("A", 1, 1, 1,),
-    ("KG", 1, 0,),
-    ("KG", 1, 1,),
-    ("Qq", 3,),
-    ("LVS", 3,),
-    ("VSg", 0,),
-    ("VSg", 1,),
-    ("A", 2, 0, 1,),
-    ("KG", 0, 1,),
-    ("L", 2, 1,),
-    ("A", 2, 1, 1,),
-    ("KG", 2, 0,),
-    ("A", 2, 1, 0,),
-    ("L", 3, 1,),
-    ("KG", 2, 1,),
-    ("IL", 0,),
-    ("Qc", 1,),
-    ("IL", 1,),
-    ("IL", 2,),
-    ("KQ", 0,),
-    ("VG", 1,),
-    ("KQ", 1,),
-    ("KG", 3, 0,),
-    ("Qq", 1,),
-    ("KQ", 2,),
-    ("VSt", 2,),
-    ("A", 3, 1, 1,),
-    ("A", 3, 1, 0,),
-    ("VT", 1,),
-    ("VSt", 1,),
-    ("KSg", 3,),
-    ("MM", 0,),
-    ("KG", 3, 1,),
-    ("MM", 1,),
-    ("VG", 3,),
-    ("VT", 3,),
-    ("VSg", 3,),
-    ("VG", 0,),
-    ("SC", 0,),
-    ("MM", 2,),
-    ("AT", 0,),
-    ("VSt", 0,),
-    ("IL", 3,),
-    ("SC", 1,),
-    ("VSt", 3,),
-    ("MAX", 0,),
-    ("VT", 2,),
-    ("AT", 1,),
-    ("VQ", 2,),
-    ("VT", 0,),
-    ("SC", 2,),
-    ("VQ", 3,),
-    ("EX", 0,),
-    ("MAX", 1,),
-    ("PT", 0,),
-    ("KSt", 3,),
-    ("EX", 1,),
-    ("WM", 0,),
-    ("PT", 1,),
-    ("KQ", 3,),
-    ("AT", 2,),
-    ("WM", 1,),
-    ("WQ", 0,),
-    ("REC", 1,),
-    ("VQ", 0,),
-    ("WQ", 1,),
-    ("MAX", 2,),
-    ("MM", 3,),
-    ("SC", 3,),
-    ("AT", 3,),
-    ("EX", 2,),
-    ("PT", 2,),
-    ("M2", 0,),
-    ("REC", 0,),
-    ("MAX", 3,),
-    ("WM", 2,),
-    ("EX", 3,),
-    ("WQ", 2,),
-    ("VQ", 1,),
-    ("PT", 3,),
-    ("Y", 0,),
-    ("REC", 2,),
-    ("M2", 2,),
-    ("WM", 3,),
-    ("Y", 2,),
-    ("M2", 1,),
-    ("Y", 1,),
-    ("WQ", 3,),
-    ("REC", 3,),
-    ("M2", 3,),
-    ("Y", 3,),
-)
 FLOPS = 2 * B * NQ * N * (D + DV)
 
 COPY = mybir.ActivationFunctionType.Copy
@@ -170,151 +28,143 @@ def tile_attend_mqa_seg_ks_kernel(tc, qT, kT, vT, ks, vs, offs, out):
     nc = tc.nc
     with ExitStack() as ctx:
         held = ctx.enter_context(tc.tile_pool(name="held", bufs=1))
-        first = ctx.enter_context(tc.tile_pool(name="first", bufs=4))
-        stage = ctx.enter_context(tc.tile_pool(name="stage", bufs=6))
-        pair = ctx.enter_context(tc.tile_pool(name="pair", bufs=4))
-        ring = ctx.enter_context(tc.tile_pool(name="ring", bufs=3))
-        work = ctx.enter_context(tc.tile_pool(name="work", bufs=4))
-        deep = ctx.enter_context(tc.tile_pool(name="deep", bufs=4))
+        two = ctx.enter_context(tc.tile_pool(name="two", bufs=2))
+        stage = ctx.enter_context(tc.tile_pool(name="stage", bufs=4))
+        four = ctx.enter_context(tc.tile_pool(name="four", bufs=4))
         psum1 = ctx.enter_context(tc.psum_pool(name="psum1", bufs=1))
         psum2 = ctx.enter_context(tc.psum_pool(name="psum2", bufs=2))
+        psum3 = ctx.enter_context(tc.psum_pool(name="psum3", bufs=3))
 
         offsets = held.tile([P, B * COLS], U16, name="offsets")
         nc.sync.dma_start(offsets[:], offs)
-
         k_pair = [held.tile([P, 2 * T], BF16, name=f"k_pair{h}") for h in range(2)]
-        v_raw = held.tile([P, T], F32, name="v_raw")
-        ks_row = held.tile([P, T], F32, name="ks_row")
-        vs_row = held.tile([P, T], F32, name="vs_row")
-        q_raw = [held.tile([P, 4, NQ], F32, name=f"q_raw{b}") for b in range(B)]
         ident = held.tile([P, P], F32, name="ident")
         ident_bf = held.tile([P, P], BF16, name="ident_bf")
         warm = held.tile([P, 1], F32, name="warm")
+        total = held.tile([P, B], F32, name="total")
+        mixed = psum1.tile([P, B, DV], F32, name="mixed")
 
         nc.vector.memset(warm[:], 0.0)
         nc.scalar.activation(warm[:], warm[:], EXP)
-        nc.vector.memset(ks_row[:, 0:SEG], 0.0)
-        nc.vector.memset(vs_row[:, 0:SEG], 0.0)
-        nc.gpsimd.memset(ks_row[:, SEG : 2 * SEG], 0.0)
+        ks_row = held.tile([P, T], F32, name="ks_row")
+        vs_row = held.tile([P, T], F32, name="vs_row")
         make_identity(nc, ident[:])
         nc.gpsimd.tensor_copy(ident_bf[:], ident[:])
-        nc.gpsimd.memset(vs_row[:, SEG : 2 * SEG], 0.0)
-        nc.gpsimd.memset(ks_row[:, 2 * SEG : T], 0.0)
-        nc.gpsimd.memset(vs_row[:, 2 * SEG : T], 0.0)
+        for half in range(2):
+            cols = slice(half * T // 2, (half + 1) * T // 2)
+            nc.vector.memset(ks_row[:, cols], 0.0)
+            nc.gpsimd.memset(vs_row[:, cols], 0.0)
+            nc.scalar.dma_start(ks_row[0:1, cols], ks[0:1, cols])
+            nc.scalar.dma_start(vs_row[0:1, cols], vs[0:1, cols])
 
-        k_raw = {}
-
-        def load_q(b):
-            nc.sync.dma_start(q_raw[b][:], qT[b].rearrange("(p j) n -> p j n", j=4))
-
-        def load_k(b, h, i=None):
-            rows = kT.rearrange("(p j) t -> p j t", j=4)
-            lo, width = (b * SEG, SEG) if i is None else (b * SEG + i * 512, 512)
-            tile = (stage if i is None else first).tile([P, 2, width], F32, name="k_raw" if i is None else "k_first")
-            nc.sync.dma_start(tile[:], rows[:, 2 * h : 2 * h + 2, lo : lo + width])
-            for j in range(lo, lo + width, 512):
-                k_raw[b, h, j // 512 % 2] = tile[:, :, j - lo : j - lo + 512]
-
-        def load_key_scales(b):
-            nc.sync.dma_start(ks_row[0:1, b * SEG : (b + 1) * SEG], ks[0:1, b * SEG : (b + 1) * SEG])
-
-        def load_value_scales(b):
-            nc.sync.dma_start(vs_row[0:1, b * SEG : (b + 1) * SEG], vs[0:1, b * SEG : (b + 1) * SEG])
-
-        def load_v(b):
-            nc.sync.dma_start(v_raw[:, b * SEG : (b + 1) * SEG], vT[:, b * SEG : (b + 1) * SEG])
-
-        def slots(b):
-            return offsets[:, b * COLS : (b + 1) * COLS]
-
-        def quantize(x_bf, width, pool, name):
-            codes = pool.tile([P, width], U32, align_bytes=64, name=f"{name}_codes")
-            scales = pool.tile([P, width], U8, align_bytes=64, name=f"{name}_scales")
-            nc.vector.quantize_mx(out=codes[:].bitcast(FP8X4), scales=scales[:], in_=x_bf)
+        def quantize(values_bf, width, name):
+            codes = four.tile([P, width], U32, align_bytes=64, name=f"{name}_codes")
+            scales = four.tile([P, width], U8, align_bytes=64, name=f"{name}_scales")
+            nc.vector.quantize_mx(out=codes[:].bitcast(FP8X4), scales=scales[:], in_=values_bf)
             return codes, scales
 
-        q, ks_col, vs_col = {}, {}, {}
-        k_mx, scaled, prob, total, v_got, v_bf, v_mx, w_bf, w_mx = {}, {}, {}, {}, {}, {}, {}, {}, {}
+        rows = kT.rearrange("(p j) t -> p j t", j=4)
+        raws = {}
+        for b in range(B):
+            for h in range(2):
+                raw = stage.tile([P, 2, SEG], F32, name="table")
+                step = HALF if b == 0 else SEG
+                for lo in range(0, SEG, step):
+                    nc.sync.dma_start(
+                        raw[:, :, lo : lo + step],
+                        rows[:, 2 * h : 2 * h + 2, b * SEG + lo : b * SEG + lo + step],
+                    )
+                raws[b, h] = raw
+        q_raw = stage.tile([P, B, 4, NQ], F32, name="table")
+        for b in range(B):
+            nc.sync.dma_start(q_raw[:, b, :, :], qT[b].rearrange("(p j) n -> p j n", j=4))
+        v_raw = stage.tile([P, T], F32, name="table")
+        for half in range(2):
+            cols = slice(half * T // 2, (half + 1) * T // 2)
+            nc.sync.dma_start(v_raw[:, cols], vT[:, cols])
 
-        q_bfs = {}
-
-        def cast_queries(b):
-            q_bf = q_bfs[b] = deep.tile([P, NQ, 4], BF16, align_bytes=64, name="q_bf")
-            src = q_raw[b][:].rearrange("p j n -> p n j")
-            if b in Q_ON_G:
-                nc.gpsimd.tensor_scalar(q_bf[:], src, 1.0, 0.0, MULT, ADD)
-            else:
-                nc.scalar.activation(q_bf[:], src, COPY)
-
-        def quantize_queries(b):
-            q_bf = q_bfs[b]
-            q[b] = quantize(q_bf[:].rearrange("p n j -> p (n j)"), NQ, deep, "q")
-
-        row_got = {}
-
-        def key_scales(b):
-            got = row_got["k", b] = pair.tile([P, N], F32, name="row_got")
-            nc.vector.tensor_copy(got[:], ks_row[:, 0 : (b + 1) * SEG].indirect(slots(b)))
-
-        def key_column(b):
-            got = row_got["k", b]
-            turned = psum1.tile([P, 4, P], F32, name="scale_turned")
-            for c in range(4):
-                nc.tensor.transpose(turned[:, c, :], got[:, c * P : (c + 1) * P], ident[:])
-            ks_col[b] = deep.tile([P, 4], F32, name="ks_col")
-            nc.scalar.activation(ks_col[b][:], turned[:, :, 0], COPY, scale=-1.0)
-
-        def value_scales(b):
-            got = row_got["v", b] = pair.tile([P, N], F32, name="row_got")
-            nc.vector.tensor_copy(got[:], vs_row[:, 0 : (b + 1) * SEG].indirect(slots(b)))
-
-        def value_column(b):
-            got = row_got["v", b]
-            turned = psum1.tile([P, 4, P], F32, name="scale_turned")
-            for t in range(4):
-                nc.tensor.transpose(turned[:, t, :], got[:, t::4], ident[:])
-            vs_col[b] = deep.tile([P, 1, 4], F32, name="vs_col")
-            nc.scalar.activation(vs_col[b][:, 0, :], turned[:, :, 0], COPY)
-
-        def cast_keys(b, h, halves=(0, 1)):
-            for i in halves:
-                c = i * 512
-                lo = 2 * (b * SEG + c)
-                copy = nc.scalar.activation if (b, h, i) not in A_ON_V else lambda o, s, f: nc.vector.tensor_copy(o, s)
-                copy(
-                    k_pair[h][:, lo : lo + 1024].rearrange("p (n e) -> p n e", e=2),
-                    k_raw[b, h, i].rearrange("p e n -> p n e"),
-                    COPY,
-                )
-
-        k_bf, all_dots, w_turned, mixes = {}, {}, {}, {}
-
-        k_got = {}
-
-        def gather_keys(b, h):
-            if h == 0:
-                k_got[b] = ring.tile([P, 2, 2 * N], BF16, align_bytes=64, name="k_got")
-            table = k_pair[h][:, 0 : 2 * (b + 1) * SEG].bitcast(U32)
-            nc.vector.tensor_copy(k_got[b][:, h, :].bitcast(U32), table.indirect(slots(b)))
-
-        def interleave(b):
-            k_bf[b] = ring.tile([P, N * 4], BF16, align_bytes=64, name="gathered")
-            if b in IL_ON_S:
-                nc.scalar.copy(
-                    k_bf[b][:].rearrange("p (n h e) -> p n h e", h=2, e=2),
-                    k_got[b][:].rearrange("p h (n e) -> p n h e", e=2),
-                )
-            else:
+        def gather_halves(out, table):
+            for half in range(2):
+                lists = slice(half * 2 * COLS, (half + 1) * 2 * COLS)
                 nc.vector.tensor_copy(
-                    k_bf[b][:].bitcast(U32).rearrange("p (n h) -> p n h", h=2),
-                    k_got[b][:].rearrange("p h x -> p (h x)").bitcast(U32).rearrange("p (h n) -> p n h", h=2),
+                    out[half], table[:, 0 : (half + 1) * T // 2].indirect(offsets[:, lists])
                 )
 
-        def quantize_keys(b):
-            k_mx[b] = quantize(k_bf[b][:], N, work, "k")
+        ks_got = two.tile([P, B * N], F32, name="got")
+        gather_halves([ks_got[:, 0 : 2 * N], ks_got[:, 2 * N : 4 * N]], ks_row)
+        vs_got = two.tile([P, B * N], F32, name="got")
+        gather_halves([vs_got[:, 0 : 2 * N], vs_got[:, 2 * N : 4 * N]], vs_row)
 
-        def scores(b):
-            k_codes, k_scales = k_mx[b]
+        k = []
+        k_got = {b: two.tile([P, 2, 2 * N], BF16, name="k_got") for b in (0, 1, 3, 2)}
+        for b in range(B):
+            got = k_got[b]
+            for h in range(2):
+                for lo in range(0, SEG, HALF):
+                    c = b * SEG + lo
+                    nc.scalar.activation(
+                        k_pair[h][:, 2 * c : 2 * (c + HALF)].rearrange("p (n e) -> p n e", e=2),
+                        raws[b, h][:, :, lo : lo + HALF].rearrange("p e n -> p n e"),
+                        COPY,
+                    )
+            for h in range(2):
+                table = k_pair[h][:, 0 : 2 * (b + 1) * SEG].bitcast(U32)
+                nc.vector.tensor_copy(
+                    got[:, h, :].bitcast(U32), table.indirect(offsets[:, b * COLS : (b + 1) * COLS])
+                )
+            k_bf = four.tile([P, N * 4], BF16, align_bytes=64, name="k_bf")
+            nc.vector.tensor_copy(
+                k_bf[:].bitcast(U32).rearrange("p (n h) -> p n h", h=2),
+                got[:].rearrange("p h x -> p (h x)").bitcast(U32).rearrange("p (h n) -> p n h", h=2),
+            )
+            k.append(quantize(k_bf[:], N, "k"))
+
+        ks_col, vs_col = [], []
+        for b in range(B):
+            turned = psum2.tile([P, 4, P], F32, name="turned")
+            for c in range(4):
+                i = 4 * b + c
+                nc.tensor.transpose(turned[:, c, :], ks_got[:, i * P : (i + 1) * P], ident[:])
+            col = four.tile([P, 4], F32, name="ks_col")
+            nc.vector.tensor_scalar_mul(col[:], turned[:, :, 0], -1.0)
+            ks_col.append(col)
+        for b in range(B):
+            turned = psum2.tile([P, 4, P], F32, name="turned")
+            for t in range(4):
+                nc.tensor.transpose(turned[:, t, :], vs_got[:, b * N + t : (b + 1) * N : 4], ident[:])
+            col = four.tile([P, 1, 4], F32, name="vs_col")
+            nc.vector.tensor_copy(col[:, 0, :], turned[:, :, 0])
+            vs_col.append(col)
+
+
+        v = []
+
+        def values(half, got):
+            nc.vector.tensor_copy(
+                got[:].rearrange("p b t s -> p b s t"),
+                v_raw[:, 0 : (half + 1) * T // 2].indirect(offsets[:, half * 2 * COLS : (half + 1) * 2 * COLS]),
+            )
+            v_bf = two.tile([P, 2, DV, 4], BF16, align_bytes=64, name="v_bf")
+            for i in range(2):
+                turned = psum2.tile([P, 4, DV], BF16, name="turned")
+                for t in range(4):
+                    nc.tensor.transpose(turned[:, t, :], got[:, i, t, :], ident_bf[:])
+                nc.scalar.copy(v_bf[:, i, :, :], turned[:].rearrange("p t e -> p e t"))
+            codes, scales = quantize(v_bf[:].rearrange("p b e t -> p (b e t)"), 2 * DV, "v")
+            for i in range(2):
+                v.append((codes[:, i * DV : (i + 1) * DV], scales[:, i * DV : (i + 1) * DV]))
+
+        q = []
+        for b in range(B):
+            q_bf = four.tile([P, NQ, 4], BF16, align_bytes=64, name="q_bf")
+            src = q_raw[:, b, :, :].rearrange("p j n -> p n j")
+            nc.scalar.activation(q_bf[:], src, COPY)
+            q.append(quantize(q_bf[:].rearrange("p n j -> p (n j)"), NQ, "q"))
+
+        scores = []
+        scaled = {b: four.tile([P, 4, NQ], F32, name="scaled") for b in reversed(range(B))}
+        for b in range(B):
+            k_codes, k_scales = k[b]
             q_codes, q_scales = q[b]
             dots = psum2.tile([P, 4, NQ], F32, name="dots")
             for c in range(4):
@@ -328,101 +178,55 @@ def tile_attend_mqa_seg_ks_kernel(tc, qT, kT, vT, ks, vs, offs, out):
                     start=True,
                     stop=True,
                 )
-            all_dots[b] = dots
-
-        def scale_scores(b):
-            dots = all_dots[b]
-            scaled[b] = work.tile([P, 4, NQ], F32, name="scaled")
+            part = scaled[b]
             for c in range(4):
-                nc.scalar.activation(scaled[b][:, c, :], dots[:, c, :], COPY, scale=ks_col[b][:, c : c + 1])
-
-        score, low = {}, {}
-
-        def turn_scores(b):
-            score[b] = psum2.tile([P, N], F32, name="score")
+                nc.scalar.activation(part[:, c, :], dots[:, c, :], COPY, scale=ks_col[b][:, c : c + 1])
+            score = psum3.tile([P, N], F32, name="score")
             for c in range(4):
-                nc.tensor.transpose(score[b][:, c * P : (c + 1) * P], scaled[b][:, c, :], ident[:])
+                nc.tensor.transpose(score[:, c * P : (c + 1) * P], part[:, c, :], ident[:])
+            scores.append(score)
 
-        def maxima(b):
-            low[b] = deep.tile([P, 1], F32, name="low")
-            nc.vector.tensor_reduce(low[b][:], score[b][:], mybir.AxisListType.X, MIN)
-
-        def exponentials(b):
-            prob[b] = work.tile([P, 4, P], F32, name="prob")
-            total[b] = deep.tile([P, 1], F32, name="total")
+        prob = []
+        for b in range(B):
+            score = scores[b]
+            low = four.tile([P, 1], F32, name="low")
+            nc.vector.tensor_reduce(low[:], score[:], mybir.AxisListType.X, MIN)
+            part = four.tile([P, 4, P], F32, name="prob")
             nc.scalar.activation(
-                prob[b][:],
-                score[b][:].rearrange("p (s t) -> p t s", t=4),
+                part[:],
+                score[:].rearrange("p (s t) -> p t s", t=4),
                 EXP,
-                bias=low[b][:],
+                bias=low[:],
                 scale=-1.0,
-                accum_out=total[b][:],
+                accum_out=total[:, b : b + 1],
             )
+            prob.append(part)
 
-        def gather_values(b):
-            v_got[b] = pair.tile([P, 4, P], BF16, name="v_got")
-            nc.vector.tensor_copy(
-                v_got[b][:].rearrange("p t s -> p s t"), v_raw[:, 0 : (b + 1) * SEG].indirect(slots(b))
-            )
+        values(0, two.tile([P, 2, 4, P], BF16, name="k_got"))
+        values(1, four.tile([P, 2, 4, P], BF16, name="scaled"))
 
-        def turn_values(b):
-            turned = psum1.tile([P, 4, DV], BF16, name="v_turned")
-            for t in range(4):
-                nc.tensor.transpose(turned[:, t, :], v_got[b][:, t, :], ident_bf[:])
-            v_bf[b] = work.tile([P, DV, 4], BF16, align_bytes=64, name="v_bf")
-            nc.scalar.copy(v_bf[b][:], turned[:].rearrange("p t e -> p e t"))
-
-        def quantize_values(b):
-            v_mx[b] = quantize(v_bf[b][:].rearrange("p e t -> p (e t)"), DV, work, "v")
-
-        def turn_weights(b):
-            turned = w_turned[b] = psum1.tile([P, 4, NQ], F32, name="w_turned")
+        for b in range(B):
+            turned = psum2.tile([P, 4, NQ], F32, name="dots")
             for t in range(4):
                 nc.tensor.transpose(turned[:, t, :], prob[b][:, t, :], ident[:])
-
-        def weigh(b):
-            turned = w_turned[b]
-            w_bf[b] = work.tile([P, NQ, 4], BF16, align_bytes=64, name="w_bf")
+            w_bf = four.tile([P, NQ, 4], BF16, align_bytes=64, name="w_bf")
             nc.vector.tensor_tensor(
-                w_bf[b][:], turned[:].rearrange("p t n -> p n t"), vs_col[b][:].to_broadcast([P, NQ, 4]), MULT
+                w_bf[:], turned[:].rearrange("p t n -> p n t"), vs_col[b][:].to_broadcast([P, NQ, 4]), MULT
             )
-
-        def quantize_weights(b):
-            w_mx[b] = quantize(w_bf[b][:].rearrange("p n t -> p (n t)"), NQ, work, "w")
-
-        def mix(b):
-            w_codes, w_scales = w_mx[b]
-            v_codes, v_scales = v_mx[b]
-            mixed = psum1.tile([P, DV], F32, name="mixed")
+            w_codes, w_scales = quantize(w_bf[:].rearrange("p n t -> p (n t)"), NQ, "w")
+            v_codes, v_scales = v[b]
             nc.tensor.matmul_mx(
-                out=mixed[:],
+                out=mixed[:, b, :],
                 lhsT=w_codes[:].bitcast(FP8X4),
                 lhsT_scale=w_scales[:],
-                rhs=v_codes[:].bitcast(FP8X4),
-                rhs_scale=v_scales[:],
+                rhs=v_codes.bitcast(FP8X4),
+                rhs_scale=v_scales,
                 start=True,
                 stop=True,
             )
-            mixes[b] = mixed
-
-        inverses = {}
-
-        def invert(b):
-            inverse = inverses[b] = deep.tile([P, 1], F32, name="inverse")
-            nc.vector.reciprocal(inverse[:], total[b][:])
-
-        def finish(b):
-            inverse, mixed = inverses[b], mixes[b]
-            y = work.tile([P, DV], F32, name="y")
-            nc.scalar.activation(y[:], mixed[:], COPY, scale=inverse[:])
+        inverse = four.tile([P, 1, B], F32, name="vs_col")
+        nc.vector.reciprocal(inverse[:, 0, :], total[:])
+        for b in range(B):
+            y = four.tile([P, DV], F32, name="y")
+            nc.scalar.activation(y[:], mixed[:, b, :], COPY, scale=inverse[:, 0, b : b + 1])
             nc.sync.dma_start(out[b], y[:])
-
-        units = {
-            "L": load_k, "LQ": load_q, "LKS": load_key_scales, "LVS": load_value_scales, "LV": load_v,
-            "Qc": cast_queries, "Qq": quantize_queries, "KSg": key_scales, "KSt": key_column, "VSg": value_scales,
-            "VSt": value_column, "A": lambda b, h, i: cast_keys(b, h, (i,)), "KG": gather_keys, "IL": interleave, "KQ": quantize_keys, "MM": scores,
-            "SC": scale_scores, "AT": turn_scores, "MAX": maxima, "EX": exponentials, "VG": gather_values, "VT": turn_values, "VQ": quantize_values, "PT": turn_weights, "WM": weigh,
-            "WQ": quantize_weights, "REC": invert, "M2": mix, "Y": finish,
-        }
-        for u in ORDER:
-            units[u[0]](*u[1:])

from contextlib import ExitStack

import concourse.mybir as mybir
from concourse.masks import make_identity

F32 = mybir.dt.float32
BF16 = mybir.dt.bfloat16
U32 = mybir.dt.uint32
U16 = mybir.dt.uint16
U8 = mybir.dt.uint8
FP8X4 = mybir.dt.float8_e4m3fn_x4

P = 128
B, N, T, D, DV, NQ = 4, 512, 4096, 512, 128, 128
SEG = T // B
HALF = SEG // 2
COLS = N // 16
FLOPS = 2 * B * NQ * N * (D + DV)

COPY = mybir.ActivationFunctionType.Copy
EXP = mybir.ActivationFunctionType.Exp
MULT = mybir.AluOpType.mult
ADD = mybir.AluOpType.add
MIN = mybir.AluOpType.min


def tile_attend_mqa_seg_ks_kernel(tc, qT, kT, vT, ks, vs, offs, out):
    nc = tc.nc
    with ExitStack() as ctx:
        held = ctx.enter_context(tc.tile_pool(name="held", bufs=1))
        two = ctx.enter_context(tc.tile_pool(name="two", bufs=2))
        stage = ctx.enter_context(tc.tile_pool(name="stage", bufs=4))
        four = ctx.enter_context(tc.tile_pool(name="four", bufs=4))
        psum1 = ctx.enter_context(tc.psum_pool(name="psum1", bufs=1))
        psum2 = ctx.enter_context(tc.psum_pool(name="psum2", bufs=2))
        psum3 = ctx.enter_context(tc.psum_pool(name="psum3", bufs=3))

        offsets = held.tile([P, B * COLS], U16, name="offsets")
        nc.sync.dma_start(offsets[:], offs)
        k_pair = [held.tile([P, 2 * T], BF16, name=f"k_pair{h}") for h in range(2)]
        ident = held.tile([P, P], F32, name="ident")
        ident_bf = held.tile([P, P], BF16, name="ident_bf")
        warm = held.tile([P, 1], F32, name="warm")
        total = held.tile([P, B], F32, name="total")
        mixed = psum1.tile([P, B, DV], F32, name="mixed")

        nc.vector.memset(warm[:], 0.0)
        nc.scalar.activation(warm[:], warm[:], EXP)
        ks_row = held.tile([P, T], F32, name="ks_row")
        vs_row = held.tile([P, T], F32, name="vs_row")
        make_identity(nc, ident[:])
        nc.gpsimd.tensor_copy(ident_bf[:], ident[:])
        for half in range(2):
            cols = slice(half * T // 2, (half + 1) * T // 2)
            nc.vector.memset(ks_row[:, cols], 0.0)
            nc.gpsimd.memset(vs_row[:, cols], 0.0)
            nc.scalar.dma_start(ks_row[0:1, cols], ks[0:1, cols])
            nc.scalar.dma_start(vs_row[0:1, cols], vs[0:1, cols])

        def quantize(values_bf, width, name):
            codes = four.tile([P, width], U32, align_bytes=64, name=f"{name}_codes")
            scales = four.tile([P, width], U8, align_bytes=64, name=f"{name}_scales")
            nc.vector.quantize_mx(out=codes[:].bitcast(FP8X4), scales=scales[:], in_=values_bf)
            return codes, scales

        rows = kT.rearrange("(p j) t -> p j t", j=4)
        raws = {}
        for b in range(B):
            for h in range(2):
                raw = stage.tile([P, 2, SEG], F32, name="table")
                step = HALF if b == 0 else SEG
                for lo in range(0, SEG, step):
                    nc.sync.dma_start(
                        raw[:, :, lo : lo + step],
                        rows[:, 2 * h : 2 * h + 2, b * SEG + lo : b * SEG + lo + step],
                    )
                raws[b, h] = raw
        q_raw = stage.tile([P, B, 4, NQ], F32, name="table")
        for b in range(B):
            nc.sync.dma_start(q_raw[:, b, :, :], qT[b].rearrange("(p j) n -> p j n", j=4))
        v_raw = stage.tile([P, T], F32, name="table")
        for half in range(2):
            cols = slice(half * T // 2, (half + 1) * T // 2)
            nc.sync.dma_start(v_raw[:, cols], vT[:, cols])

        def gather_halves(out, table):
            for half in range(2):
                lists = slice(half * 2 * COLS, (half + 1) * 2 * COLS)
                nc.vector.tensor_copy(
                    out[half], table[:, 0 : (half + 1) * T // 2].indirect(offsets[:, lists])
                )

        ks_got = two.tile([P, B * N], F32, name="got")
        gather_halves([ks_got[:, 0 : 2 * N], ks_got[:, 2 * N : 4 * N]], ks_row)
        vs_got = two.tile([P, B * N], F32, name="got")
        gather_halves([vs_got[:, 0 : 2 * N], vs_got[:, 2 * N : 4 * N]], vs_row)

        k = []
        k_got = {b: two.tile([P, 2, 2 * N], BF16, name="k_got") for b in (0, 1, 3, 2)}
        for b in range(B):
            got = k_got[b]
            for h in range(2):
                for lo in range(0, SEG, HALF):
                    c = b * SEG + lo
                    nc.scalar.activation(
                        k_pair[h][:, 2 * c : 2 * (c + HALF)].rearrange("p (n e) -> p n e", e=2),
                        raws[b, h][:, :, lo : lo + HALF].rearrange("p e n -> p n e"),
                        COPY,
                    )
            for h in range(2):
                table = k_pair[h][:, 0 : 2 * (b + 1) * SEG].bitcast(U32)
                nc.vector.tensor_copy(
                    got[:, h, :].bitcast(U32), table.indirect(offsets[:, b * COLS : (b + 1) * COLS])
                )
            k_bf = four.tile([P, N * 4], BF16, align_bytes=64, name="k_bf")
            nc.vector.tensor_copy(
                k_bf[:].bitcast(U32).rearrange("p (n h) -> p n h", h=2),
                got[:].rearrange("p h x -> p (h x)").bitcast(U32).rearrange("p (h n) -> p n h", h=2),
            )
            k.append(quantize(k_bf[:], N, "k"))

        ks_col, vs_col = [], []
        for b in range(B):
            turned = psum2.tile([P, 4, P], F32, name="turned")
            for c in range(4):
                i = 4 * b + c
                nc.tensor.transpose(turned[:, c, :], ks_got[:, i * P : (i + 1) * P], ident[:])
            col = four.tile([P, 4], F32, name="ks_col")
            nc.vector.tensor_scalar_mul(col[:], turned[:, :, 0], -1.0)
            ks_col.append(col)
        for b in range(B):
            turned = psum2.tile([P, 4, P], F32, name="turned")
            for t in range(4):
                nc.tensor.transpose(turned[:, t, :], vs_got[:, b * N + t : (b + 1) * N : 4], ident[:])
            col = four.tile([P, 1, 4], F32, name="vs_col")
            nc.vector.tensor_copy(col[:, 0, :], turned[:, :, 0])
            vs_col.append(col)


        v = []

        def values(half, got):
            nc.vector.tensor_copy(
                got[:].rearrange("p b t s -> p b s t"),
                v_raw[:, 0 : (half + 1) * T // 2].indirect(offsets[:, half * 2 * COLS : (half + 1) * 2 * COLS]),
            )
            v_bf = two.tile([P, 2, DV, 4], BF16, align_bytes=64, name="v_bf")
            for i in range(2):
                turned = psum2.tile([P, 4, DV], BF16, name="turned")
                for t in range(4):
                    nc.tensor.transpose(turned[:, t, :], got[:, i, t, :], ident_bf[:])
                nc.scalar.copy(v_bf[:, i, :, :], turned[:].rearrange("p t e -> p e t"))
            codes, scales = quantize(v_bf[:].rearrange("p b e t -> p (b e t)"), 2 * DV, "v")
            for i in range(2):
                v.append((codes[:, i * DV : (i + 1) * DV], scales[:, i * DV : (i + 1) * DV]))

        q = []
        for b in range(B):
            q_bf = four.tile([P, NQ, 4], BF16, align_bytes=64, name="q_bf")
            src = q_raw[:, b, :, :].rearrange("p j n -> p n j")
            nc.scalar.activation(q_bf[:], src, COPY)
            q.append(quantize(q_bf[:].rearrange("p n j -> p (n j)"), NQ, "q"))

        scores = []
        scaled = {b: four.tile([P, 4, NQ], F32, name="scaled") for b in reversed(range(B))}
        for b in range(B):
            k_codes, k_scales = k[b]
            q_codes, q_scales = q[b]
            dots = psum2.tile([P, 4, NQ], F32, name="dots")
            for c in range(4):
                cols = slice(c * P, (c + 1) * P)
                nc.tensor.matmul_mx(
                    out=dots[:, c, :],
                    lhsT=k_codes[:, cols].bitcast(FP8X4),
                    lhsT_scale=k_scales[:, cols],
                    rhs=q_codes[:].bitcast(FP8X4),
                    rhs_scale=q_scales[:],
                    start=True,
                    stop=True,
                )
            part = scaled[b]
            for c in range(4):
                nc.scalar.activation(part[:, c, :], dots[:, c, :], COPY, scale=ks_col[b][:, c : c + 1])
            score = psum3.tile([P, N], F32, name="score")
            for c in range(4):
                nc.tensor.transpose(score[:, c * P : (c + 1) * P], part[:, c, :], ident[:])
            scores.append(score)

        prob = []
        for b in range(B):
            score = scores[b]
            low = four.tile([P, 1], F32, name="low")
            nc.vector.tensor_reduce(low[:], score[:], mybir.AxisListType.X, MIN)
            part = four.tile([P, 4, P], F32, name="prob")
            nc.scalar.activation(
                part[:],
                score[:].rearrange("p (s t) -> p t s", t=4),
                EXP,
                bias=low[:],
                scale=-1.0,
                accum_out=total[:, b : b + 1],
            )
            prob.append(part)

        values(0, two.tile([P, 2, 4, P], BF16, name="k_got"))
        values(1, four.tile([P, 2, 4, P], BF16, name="scaled"))

        for b in range(B):
            turned = psum2.tile([P, 4, NQ], F32, name="dots")
            for t in range(4):
                nc.tensor.transpose(turned[:, t, :], prob[b][:, t, :], ident[:])
            w_bf = four.tile([P, NQ, 4], BF16, align_bytes=64, name="w_bf")
            nc.vector.tensor_tensor(
                w_bf[:], turned[:].rearrange("p t n -> p n t"), vs_col[b][:].to_broadcast([P, NQ, 4]), MULT
            )
            w_codes, w_scales = quantize(w_bf[:].rearrange("p n t -> p (n t)"), NQ, "w")
            v_codes, v_scales = v[b]
            nc.tensor.matmul_mx(
                out=mixed[:, b, :],
                lhsT=w_codes[:].bitcast(FP8X4),
                lhsT_scale=w_scales[:],
                rhs=v_codes.bitcast(FP8X4),
                rhs_scale=v_scales,
                start=True,
                stop=True,
            )
        inverse = four.tile([P, 1, B], F32, name="vs_col")
        nc.vector.reciprocal(inverse[:, 0, :], total[:])
        for b in range(B):
            y = four.tile([P, DV], F32, name="y")
            nc.scalar.activation(y[:], mixed[:, b, :], COPY, scale=inverse[:, 0, b : b + 1])
            nc.sync.dma_start(out[b], y[:])
